import numpy as np
import ml_dtypes


def mxq(x, axis, fmt="e4m3"):
    dtype, down = {"e4m3": (ml_dtypes.float8_e4m3fn, 7), "e5m2": (ml_dtypes.float8_e5m2, 14)}[fmt]
    v = np.moveaxis(np.asarray(x, np.float32).astype(ml_dtypes.bfloat16).astype(np.float64), axis, -1)
    blocks = v.reshape(v.shape[:-1] + (-1, 32))
    amax = np.abs(blocks).max(-1, keepdims=True)
    byte = np.maximum(np.where(amax > 0, np.frexp(amax)[1] - 1 + 127, 0) - down, 1)
    scale = np.exp2(byte - 127.0)
    codes = (blocks / scale).astype(np.float32).astype(dtype).astype(np.float64)
    return np.moveaxis((codes * scale).reshape(v.shape), -1, axis)


WIDE = False


def mx_kscale(k):
    if not WIDE:
        return np.ones(k)
    levels = np.array([10, -10, 5, -5, 0])
    if k % 512:
        return np.exp2(np.random.permutation(np.resize(levels, k // 32))).repeat(32)
    a = np.empty((k // 512, 16))
    for p in range(k // 512):
        a[p, :8] = np.random.permutation(np.resize(levels, 8))
        for g in range(8):
            far = levels[np.abs(levels - a[p, g]) >= 10]
            a[p, g + 8] = far[np.random.randint(len(far))]
    return np.exp2(a.ravel()).repeat(32)


def f64(x):
    return np.asarray(x).astype(np.float64)


def striped(idx):
    return np.tile(np.asarray(idx).reshape(-1, 16).T, (8, 1)).astype(np.uint16)


def unstriped(offs):
    return offs[:16].T.reshape(-1).astype(np.int64)


E2M1 = np.array([0.0, 0.5, 1.0, 1.5, 2.0, 3.0, 4.0, 6.0, -0.0, -0.5, -1.0, -1.5, -2.0, -3.0, -4.0, -6.0])


def pack_weight(w, fmt):
    k, n = w.shape
    w = f64(np.asarray(w, np.float32).astype(ml_dtypes.bfloat16)).reshape(k // 32, 32, n)
    amax = np.abs(w).max(1)
    if fmt == "e4m3":
        byte = np.frexp(amax)[1] - 1 + 127 - 7
    else:
        mant, ex = np.frexp(amax / 6.0)
        byte = np.where(mant > 0.5, ex, ex - 1) + 127
    byte = np.clip(np.where(amax > 0, byte, 1), 1, 254)
    scaled = (w * np.exp2(127.0 - byte)[:, None, :]).reshape(k, n).astype(np.float32)
    by_word = np.ascontiguousarray(scaled.reshape(k // 512, 128, 4, n).transpose(0, 1, 3, 2))
    if fmt == "e4m3":
        words = by_word.astype(ml_dtypes.float8_e4m3fn).view(np.uint8)
    else:
        c = by_word.astype(ml_dtypes.float4_e2m1fn).view(np.uint8) & 0xF
        words = (c[..., 0::2] | (c[..., 1::2] << 4)).reshape(k // 512, 128, 2 * n)
    return np.ascontiguousarray(words), np.ascontiguousarray(byte.astype(np.uint8).reshape(k // 512, 16, n))


def unpack_weight(words, scales, fmt):
    g, _, n = scales.shape
    words = np.ascontiguousarray(words).reshape(g, 128, n, -1)
    if fmt == "e4m3":
        vals = words.view(ml_dtypes.float8_e4m3fn).astype(np.float64)
    else:
        nib = np.empty((g, 128, n, 4), np.uint8)
        nib[..., 0::2] = words & 0xF
        nib[..., 1::2] = words >> 4
        vals = E2M1[nib]
    vals = vals * np.repeat(np.exp2(scales.astype(np.float64) - 127.0), 8, axis=1)[..., None]
    return vals.transpose(0, 1, 3, 2).reshape(g * 512, n)


D, E, T, I, Q = 512, 512, 2048, 512, 128


def setup_inputs():
    n = np.random.standard_normal
    idx = np.random.permutation(T)[:I]
    fd = mx_kscale(D)
    fe = mx_kscale(E)
    keysp = pack_weight(n((D, T)) / fd[:, None], "e4m3")
    valsp = pack_weight(n((E, T)) / fe[:, None], "e4m3")
    return {
        "query": (n((D, Q)) * 0.5 / np.sqrt(D) * fd[:, None]).astype(np.float32),
        "keys_words": keysp[0],
        "keys_scales": keysp[1],
        "counts": (np.random.uniform(0.0, 2.0, (Q, T))).astype(np.float32),
        "weary": (np.random.uniform(0.3, 1.0, (Q, 1))).astype(np.float32),
        "gout": (n((E, Q)) * 1 / np.sqrt(E) * fe[:, None]).astype(np.float32),
        "vals_words": valsp[0],
        "vals_scales": valsp[1],
        "lse": (np.random.uniform(5.6, 6.0, (Q, 1))).astype(np.float32),
        "delta": (np.random.uniform(-0.3, 0.3, (Q, 1))).astype(np.float32),
        "later": (0.5 * n((Q, T))).astype(np.float32),
        "offs": striped(idx),
    }


def reference(query, keys_words, keys_scales, counts, weary, gout, vals_words, vals_scales, lse, delta, later, offs):
    idx = unstriped(offs)
    keysu = unpack_weight(keys_words, keys_scales, "e4m3")
    valsu = unpack_weight(vals_words, vals_scales, "e4m3")
    queryq = mxq(f64(query), 0, "e4m3")
    keysidxg = keysu[:, idx]
    a = queryq.T @ keysidxg
    goutq = mxq(f64(gout), 0, "e4m3")
    valsidxg = valsu[:, idx]
    dp = goutq.T @ valsidxg
    ds = np.exp(a - f64(counts)[:, idx] * f64(weary) - f64(lse)) * (dp - f64(delta)) * f64(weary) * (-512.0)
    df = np.zeros((Q, T))
    df[:, idx] = ds
    y = f64(later) + df
    return y

@@ -1,0 +1,125 @@
+from contextlib import ExitStack
+
+import concourse.mybir as mybir
+
+D, E, T, I, Q = 512, 512, 2048, 512, 128
+FLOPS = 2 * Q * I * (D + E)
+
+F32 = mybir.dt.float32
+BF16 = mybir.dt.bfloat16
+I32 = mybir.dt.int32
+U32 = mybir.dt.uint32
+U16 = mybir.dt.uint16
+U8 = mybir.dt.uint8
+FP8X4 = mybir.dt.float8_e4m3fn_x4
+ALU = mybir.AluOpType
+ACT = mybir.ActivationFunctionType
+
+P = 128
+PACK = 4
+HALF = I // 2
+VALS_ROW = 4
+STORE_WIDTHS = (512, 512, 512, 512)
+
+
+def tile_attend_gweariness_kernel(tc, query, keys_words, keys_scales, counts, weary, gout, vals_words, vals_scales, lse, delta, later, offs, out):
+    nc = tc.nc
+
+    with ExitStack() as ctx:
+        keep = ctx.enter_context(tc.tile_pool(name="keep", bufs=1))
+        psum = ctx.enter_context(tc.psum_pool(name="psum", bufs=1))
+
+        offsets = keep.tile([P, I // 16], U16, name="offsets")
+        nc.sync.dma_start(offsets[:], offs)
+
+        key_bytes = keep.tile([P, T], U8, name="key_bytes", align_bytes=64)
+        val_bytes = keep.tile([P, T], U8, name="val_bytes", align_bytes=64)
+        df = keep.tile([P, T], F32, name="df")
+        nc.vector.memset(key_bytes[:].bitcast(I32), 0)
+        nc.vector.memset(val_bytes[:].bitcast(I32), 0)
+        nc.vector.memset(df[:], 0.0)
+
+        for r in range(4):
+            nc.scalar.dma_start(key_bytes[r:P:32, :].bitcast(I32), keys_scales[0, r:16:4, :].bitcast(I32))
+        for r in range(4):
+            nc.gpsimd.dma_start(val_bytes[VALS_ROW + r : P : 32, :].bitcast(I32), vals_scales[0, r:16:4, :].bitcast(I32))
+
+        weary_col = keep.tile([P, 1], F32, name="weary_col")
+        lse_col = keep.tile([P, 1], F32, name="lse_col")
+        delta_col = keep.tile([P, 1], F32, name="delta_col")
+        nc.gpsimd.dma_start(weary_col[:], weary)
+        nc.gpsimd.dma_start(lse_col[:], lse)
+        nc.gpsimd.dma_start(delta_col[:], delta)
+
+        query_raw = keep.tile([P, PACK, Q], F32, name="query_raw")
+        gout_raw = keep.tile([P, PACK, Q], F32, name="gout_raw")
+        key_words = keep.tile([P, T], U32, name="key_words", tag="keys_then_later", align_bytes=64)
+        val_words = keep.tile([P, T], U32, name="val_words", align_bytes=64)
+        counts_all = keep.tile([P, T], F32, name="counts_all")
+        nc.sync.dma_start(query_raw[:], query.rearrange("(p j) q -> p j q", j=PACK))
+        nc.sync.dma_start(key_words[:].bitcast(I32), keys_words[0].rearrange("p n t -> p (n t)").bitcast(I32))
+        nc.sync.dma_start(counts_all[:], counts)
+        nc.sync.dma_start(gout_raw[:], gout.rearrange("(p j) q -> p j q", j=PACK))
+        nc.sync.dma_start(val_words[:].bitcast(I32), vals_words[0].rearrange("p n t -> p (n t)").bitcast(I32))
+
+        def quantise(raw, name):
+            grouped = keep.tile([P, Q, PACK], BF16, name=name + "_grouped", align_bytes=64)
+            codes = keep.tile([P, Q], U32, name=name + "_codes", align_bytes=64)
+            scales = keep.tile([P, Q], U8, name=name + "_scales", align_bytes=64)
+            nc.scalar.copy(grouped[:], raw[:].rearrange("p j q -> p q j"))
+            nc.vector.quantize_mx(out=codes[:].bitcast(FP8X4), scales=scales[:], in_=grouped[:].rearrange("p q j -> p (q j)"))
+            return codes, scales
+
+        key_bytes_g = keep.tile([P, I], U8, name="key_bytes_g", align_bytes=64)
+        key_words_g = keep.tile([P, I], U32, name="key_words_g", align_bytes=64)
+        val_bytes_g = keep.tile([P, I], U8, name="val_bytes_g", align_bytes=64)
+        counts_g = keep.tile([P, I], F32, name="counts_g")
+        nc.vector.tensor_copy(key_bytes_g[:], key_bytes[:].indirect(offsets[:]))
+        query_codes, query_scales = quantise(query_raw, "query")
+        nc.vector.tensor_copy(key_words_g[:], key_words[:].indirect(offsets[:]))
+        scores = psum.tile([P, I], F32, name="scores")
+        nc.tensor.matmul_mx(out=scores[:], lhsT=query_codes[:].bitcast(FP8X4), lhsT_scale=query_scales[:],
+                            rhs=key_words_g[:].bitcast(FP8X4), rhs_scale=key_bytes_g[:], start=True, stop=True)
+
+        later_all = keep.tile([P, T], F32, name="later_all", tag="keys_then_later", align_bytes=64)
+        nc.sync.dma_start(later_all[:], later)
+
+        nc.vector.tensor_copy(val_bytes_g[:], val_bytes[:].indirect(offsets[:]))
+        nc.vector.tensor_copy(counts_g[:], counts_all[:].indirect(offsets[:]))
+        gout_codes, gout_scales = quantise(gout_raw, "gout")
+
+        neg_lse = keep.tile([P, 1], F32, name="neg_lse")
+        factor = keep.tile([P, 1], F32, name="factor")
+        neg_delta = keep.tile([P, 1], F32, name="neg_delta")
+        shift = keep.tile([P, 1], F32, name="shift")
+        nc.scalar.mul(neg_lse[:], lse_col[:], -1.0)
+        nc.scalar.mul(factor[:], weary_col[:], -512.0)
+        nc.scalar.mul(neg_delta[:], delta_col[:], -1.0)
+        nc.scalar.mul(shift[:], neg_delta[:], factor[:])
+
+        neg_logit = keep.tile([P, I], F32, name="neg_logit")
+        weights = keep.tile([P, I], F32, name="weights")
+        nc.vector.scalar_tensor_tensor(neg_logit[:], counts_g[:], weary_col[:], scores[:], ALU.mult, ALU.subtract)
+        nc.scalar.activation(weights[:], neg_logit[:], ACT.Exp, bias=neg_lse[:], scale=-1.0)
+
+        grads = []
+        for h in range(2):
+            val_words_g = keep.tile([P, HALF], U32, name="val_words_g%d" % h, align_bytes=64)
+            nc.vector.tensor_copy(val_words_g[:], val_words[:].indirect(offsets[:, h * 16 : (h + 1) * 16]))
+            dp = psum.tile([P, HALF], F32, name="dp%d" % h)
+            nc.tensor.matmul_mx(out=dp[:], lhsT=gout_codes[:].bitcast(FP8X4), lhsT_scale=gout_scales[:],
+                                rhs=val_words_g[:].bitcast(FP8X4), rhs_scale=val_bytes_g[VALS_ROW:P, h * HALF : (h + 1) * HALF],
+                                start=True, stop=True)
+            grad = keep.tile([P, HALF], F32, name="grad%d" % h)
+            nc.scalar.activation(grad[:], dp[:], ACT.Identity, bias=shift[:], scale=factor[:])
+            grads.append(grad)
+        for h in range(2):
+            nc.vector.tensor_tensor(df[:].indirect(offsets[:, h * 16 : (h + 1) * 16]), weights[:, h * HALF : (h + 1) * HALF], grads[h][:], ALU.mult)
+
+        start = 0
+        for c, width in enumerate(STORE_WIDTHS):
+            cols = slice(start, start + width)
+            result = keep.tile([P, width], F32, name="result%d" % c)
+            nc.vector.tensor_tensor(result[:], later_all[:, cols], df[:, cols], ALU.add)
+            nc.sync.dma_start(out[:, cols], result[:])
+            start += width

@@ -33,16 +33,11 @@ def tile_attend_gweariness_kernel(tc, query, keys_words, keys_scales, counts, we
         nc.sync.dma_start(offsets[:], offs)
 
         key_bytes = keep.tile([P, T], U8, name="key_bytes", align_bytes=64)
-        val_bytes = keep.tile([P, T], U8, name="val_bytes", align_bytes=64)
         df = keep.tile([P, T], F32, name="df")
         nc.vector.memset(key_bytes[:].bitcast(I32), 0)
-        nc.vector.memset(val_bytes[:].bitcast(I32), 0)
-        nc.vector.memset(df[:], 0.0)
 
         for r in range(4):
             nc.scalar.dma_start(key_bytes[r:P:32, :].bitcast(I32), keys_scales[0, r:16:4, :].bitcast(I32))
-        for r in range(4):
-            nc.gpsimd.dma_start(val_bytes[VALS_ROW + r : P : 32, :].bitcast(I32), vals_scales[0, r:16:4, :].bitcast(I32))
 
         weary_col = keep.tile([P, 1], F32, name="weary_col")
         lse_col = keep.tile([P, 1], F32, name="lse_col")
@@ -51,32 +46,43 @@ def tile_attend_gweariness_kernel(tc, query, keys_words, keys_scales, counts, we
         nc.gpsimd.dma_start(lse_col[:], lse)
         nc.gpsimd.dma_start(delta_col[:], delta)
 
-        query_raw = keep.tile([P, PACK, Q], F32, name="query_raw")
-        gout_raw = keep.tile([P, PACK, Q], F32, name="gout_raw")
+        query_raw = keep.tile([P, PACK, Q], F32, name="query_raw", tag="query_then_counts")
+        gout_raw = keep.tile([P, PACK, Q], F32, name="gout_raw", tag="gout_then_val_bytes", align_bytes=64)
         key_words = keep.tile([P, T], U32, name="key_words", tag="keys_then_later", align_bytes=64)
-        val_words = keep.tile([P, T], U32, name="val_words", align_bytes=64)
-        counts_all = keep.tile([P, T], F32, name="counts_all")
         nc.sync.dma_start(query_raw[:], query.rearrange("(p j) q -> p j q", j=PACK))
-        nc.sync.dma_start(key_words[:].bitcast(I32), keys_words[0].rearrange("p n t -> p (n t)").bitcast(I32))
-        nc.sync.dma_start(counts_all[:], counts)
         nc.sync.dma_start(gout_raw[:], gout.rearrange("(p j) q -> p j q", j=PACK))
-        nc.sync.dma_start(val_words[:].bitcast(I32), vals_words[0].rearrange("p n t -> p (n t)").bitcast(I32))
+        nc.sync.dma_start(key_words[:].bitcast(I32), keys_words[0].rearrange("p n t -> p (n t)").bitcast(I32))
 
-        def quantise(raw, name):
-            grouped = keep.tile([P, Q, PACK], BF16, name=name + "_grouped", align_bytes=64)
+        def cast(raw, name, tag):
+            grouped = keep.tile([P, Q, PACK], BF16, name=name + "_grouped", tag=tag, align_bytes=64)
+            nc.vector.tensor_copy(grouped[:], raw[:].rearrange("p j q -> p q j"))
+            return grouped
+
+        def quantise(grouped, name):
             codes = keep.tile([P, Q], U32, name=name + "_codes", align_bytes=64)
             scales = keep.tile([P, Q], U8, name=name + "_scales", align_bytes=64)
-            nc.scalar.copy(grouped[:], raw[:].rearrange("p j q -> p q j"))
             nc.vector.quantize_mx(out=codes[:].bitcast(FP8X4), scales=scales[:], in_=grouped[:].rearrange("p q j -> p (q j)"))
             return codes, scales
 
+        query_grouped = cast(query_raw, "query", "query_grouped")
+        counts_all = keep.tile([P, T], F32, name="counts_all", tag="query_then_counts")
+        nc.sync.dma_start(counts_all[:], counts)
+
+        gout_grouped = cast(gout_raw, "gout", "grouped_then_vals")
+        val_bytes = keep.tile([P, T], U8, name="val_bytes", tag="gout_then_val_bytes", align_bytes=64)
+        nc.vector.memset(val_bytes[:].bitcast(I32), 0)
+        for r in range(4):
+            nc.sync.dma_start(val_bytes[VALS_ROW + r : P : 32, :].bitcast(I32), vals_scales[0, r:16:4, :].bitcast(I32))
+        gout_codes, gout_scales = quantise(gout_grouped, "gout")
+        val_words = keep.tile([P, T], U32, name="val_words", tag="grouped_then_vals", align_bytes=64)
+        nc.sync.dma_start(val_words[:].bitcast(I32), vals_words[0].rearrange("p n t -> p (n t)").bitcast(I32))
+        query_codes, query_scales = quantise(query_grouped, "query")
+
         key_bytes_g = keep.tile([P, I], U8, name="key_bytes_g", align_bytes=64)
         key_words_g = keep.tile([P, I], U32, name="key_words_g", align_bytes=64)
-        val_bytes_g = keep.tile([P, I], U8, name="val_bytes_g", align_bytes=64)
         counts_g = keep.tile([P, I], F32, name="counts_g")
-        nc.vector.tensor_copy(key_bytes_g[:], key_bytes[:].indirect(offsets[:]))
-        query_codes, query_scales = quantise(query_raw, "query")
         nc.vector.tensor_copy(key_words_g[:], key_words[:].indirect(offsets[:]))
+        nc.vector.tensor_copy(key_bytes_g[:], key_bytes[:].indirect(offsets[:]))
         scores = psum.tile([P, I], F32, name="scores")
         nc.tensor.matmul_mx(out=scores[:], lhsT=query_codes[:].bitcast(FP8X4), lhsT_scale=query_scales[:],
                             rhs=key_words_g[:].bitcast(FP8X4), rhs_scale=key_bytes_g[:], start=True, stop=True)
@@ -84,9 +90,7 @@ def tile_attend_gweariness_kernel(tc, query, keys_words, keys_scales, counts, we
         later_all = keep.tile([P, T], F32, name="later_all", tag="keys_then_later", align_bytes=64)
         nc.sync.dma_start(later_all[:], later)
 
-        nc.vector.tensor_copy(val_bytes_g[:], val_bytes[:].indirect(offsets[:]))
         nc.vector.tensor_copy(counts_g[:], counts_all[:].indirect(offsets[:]))
-        gout_codes, gout_scales = quantise(gout_raw, "gout")
 
         neg_lse = keep.tile([P, 1], F32, name="neg_lse")
         factor = keep.tile([P, 1], F32, name="factor")
@@ -102,13 +106,21 @@ def tile_attend_gweariness_kernel(tc, query, keys_words, keys_scales, counts, we
         nc.vector.scalar_tensor_tensor(neg_logit[:], counts_g[:], weary_col[:], scores[:], ALU.mult, ALU.subtract)
         nc.scalar.activation(weights[:], neg_logit[:], ACT.Exp, bias=neg_lse[:], scale=-1.0)
 
+        for c in range(4):
+            nc.vector.memset(df[:, c * 512 : (c + 1) * 512], 0.0)
+
         grads = []
         for h in range(2):
-            val_words_g = keep.tile([P, HALF], U32, name="val_words_g%d" % h, align_bytes=64)
-            nc.vector.tensor_copy(val_words_g[:], val_words[:].indirect(offsets[:, h * 16 : (h + 1) * 16]))
+            half_offsets = offsets[:, h * 16 : (h + 1) * 16]
+            words_tag = ("first_words_then_second_bytes", "second_words")[h]
+            bytes_tag = ("first_bytes", "first_words_then_second_bytes")[h]
+            val_words_g = keep.tile([P, HALF], U32, name="val_words_g%d" % h, tag=words_tag, align_bytes=64)
+            val_bytes_g = keep.tile([P, HALF], U8, name="val_bytes_g%d" % h, tag=bytes_tag, align_bytes=64)
+            nc.vector.tensor_copy(val_words_g[:], val_words[:].indirect(half_offsets))
+            nc.vector.tensor_copy(val_bytes_g[:], val_bytes[:].indirect(half_offsets))
             dp = psum.tile([P, HALF], F32, name="dp%d" % h)
             nc.tensor.matmul_mx(out=dp[:], lhsT=gout_codes[:].bitcast(FP8X4), lhsT_scale=gout_scales[:],
-                                rhs=val_words_g[:].bitcast(FP8X4), rhs_scale=val_bytes_g[VALS_ROW:P, h * HALF : (h + 1) * HALF],
+                                rhs=val_words_g[:].bitcast(FP8X4), rhs_scale=val_bytes_g[VALS_ROW:P, :],
                                 start=True, stop=True)
             grad = keep.tile([P, HALF], F32, name="grad%d" % h)
             nc.scalar.activation(grad[:], dp[:], ACT.Identity, bias=shift[:], scale=factor[:])

from contextlib import ExitStack

import concourse.mybir as mybir

D, E, T, I, Q = 512, 512, 2048, 512, 128
FLOPS = 2 * Q * I * (D + E)

F32 = mybir.dt.float32
BF16 = mybir.dt.bfloat16
I32 = mybir.dt.int32
U32 = mybir.dt.uint32
U16 = mybir.dt.uint16
U8 = mybir.dt.uint8
FP8X4 = mybir.dt.float8_e4m3fn_x4
ALU = mybir.AluOpType
ACT = mybir.ActivationFunctionType

P = 128
PACK = 4
HALF = I // 2
VALS_ROW = 4
STORE_WIDTHS = (512, 512, 512, 512)


def tile_attend_gweariness_kernel(tc, query, keys_words, keys_scales, counts, weary, gout, vals_words, vals_scales, lse, delta, later, offs, out):
    nc = tc.nc

    with ExitStack() as ctx:
        keep = ctx.enter_context(tc.tile_pool(name="keep", bufs=1))
        psum = ctx.enter_context(tc.psum_pool(name="psum", bufs=1))

        offsets = keep.tile([P, I // 16], U16, name="offsets")
        nc.sync.dma_start(offsets[:], offs)

        key_bytes = keep.tile([P, T], U8, name="key_bytes", align_bytes=64)
        df = keep.tile([P, T], F32, name="df")
        nc.vector.memset(key_bytes[:].bitcast(I32), 0)

        for r in range(4):
            nc.scalar.dma_start(key_bytes[r:P:32, :].bitcast(I32), keys_scales[0, r:16:4, :].bitcast(I32))

        weary_col = keep.tile([P, 1], F32, name="weary_col")
        lse_col = keep.tile([P, 1], F32, name="lse_col")
        delta_col = keep.tile([P, 1], F32, name="delta_col")
        nc.gpsimd.dma_start(weary_col[:], weary)
        nc.gpsimd.dma_start(lse_col[:], lse)
        nc.gpsimd.dma_start(delta_col[:], delta)

        query_raw = keep.tile([P, PACK, Q], F32, name="query_raw", tag="query_then_counts")
        gout_raw = keep.tile([P, PACK, Q], F32, name="gout_raw", tag="gout_then_val_bytes", align_bytes=64)
        key_words = keep.tile([P, T], U32, name="key_words", tag="keys_then_later", align_bytes=64)
        nc.sync.dma_start(query_raw[:], query.rearrange("(p j) q -> p j q", j=PACK))
        nc.sync.dma_start(gout_raw[:], gout.rearrange("(p j) q -> p j q", j=PACK))
        nc.sync.dma_start(key_words[:].bitcast(I32), keys_words[0].rearrange("p n t -> p (n t)").bitcast(I32))

        def cast(raw, name, tag):
            grouped = keep.tile([P, Q, PACK], BF16, name=name + "_grouped", tag=tag, align_bytes=64)
            nc.vector.tensor_copy(grouped[:], raw[:].rearrange("p j q -> p q j"))
            return grouped

        def quantise(grouped, name):
            codes = keep.tile([P, Q], U32, name=name + "_codes", align_bytes=64)
            scales = keep.tile([P, Q], U8, name=name + "_scales", align_bytes=64)
            nc.vector.quantize_mx(out=codes[:].bitcast(FP8X4), scales=scales[:], in_=grouped[:].rearrange("p q j -> p (q j)"))
            return codes, scales

        query_grouped = cast(query_raw, "query", "query_grouped")
        counts_all = keep.tile([P, T], F32, name="counts_all", tag="query_then_counts")
        nc.sync.dma_start(counts_all[:], counts)

        gout_grouped = cast(gout_raw, "gout", "grouped_then_vals")
        val_bytes = keep.tile([P, T], U8, name="val_bytes", tag="gout_then_val_bytes", align_bytes=64)
        nc.vector.memset(val_bytes[:].bitcast(I32), 0)
        for r in range(4):
            nc.sync.dma_start(val_bytes[VALS_ROW + r : P : 32, :].bitcast(I32), vals_scales[0, r:16:4, :].bitcast(I32))
        gout_codes, gout_scales = quantise(gout_grouped, "gout")
        val_words = keep.tile([P, T], U32, name="val_words", tag="grouped_then_vals", align_bytes=64)
        nc.sync.dma_start(val_words[:].bitcast(I32), vals_words[0].rearrange("p n t -> p (n t)").bitcast(I32))
        query_codes, query_scales = quantise(query_grouped, "query")

        key_bytes_g = keep.tile([P, I], U8, name="key_bytes_g", align_bytes=64)
        key_words_g = keep.tile([P, I], U32, name="key_words_g", align_bytes=64)
        counts_g = keep.tile([P, I], F32, name="counts_g")
        nc.vector.tensor_copy(key_words_g[:], key_words[:].indirect(offsets[:]))
        nc.vector.tensor_copy(key_bytes_g[:], key_bytes[:].indirect(offsets[:]))
        scores = psum.tile([P, I], F32, name="scores")
        nc.tensor.matmul_mx(out=scores[:], lhsT=query_codes[:].bitcast(FP8X4), lhsT_scale=query_scales[:],
                            rhs=key_words_g[:].bitcast(FP8X4), rhs_scale=key_bytes_g[:], start=True, stop=True)

        later_all = keep.tile([P, T], F32, name="later_all", tag="keys_then_later", align_bytes=64)
        nc.sync.dma_start(later_all[:], later)

        nc.vector.tensor_copy(counts_g[:], counts_all[:].indirect(offsets[:]))

        neg_lse = keep.tile([P, 1], F32, name="neg_lse")
        factor = keep.tile([P, 1], F32, name="factor")
        neg_delta = keep.tile([P, 1], F32, name="neg_delta")
        shift = keep.tile([P, 1], F32, name="shift")
        nc.scalar.mul(neg_lse[:], lse_col[:], -1.0)
        nc.scalar.mul(factor[:], weary_col[:], -512.0)
        nc.scalar.mul(neg_delta[:], delta_col[:], -1.0)
        nc.scalar.mul(shift[:], neg_delta[:], factor[:])

        neg_logit = keep.tile([P, I], F32, name="neg_logit")
        weights = keep.tile([P, I], F32, name="weights")
        nc.vector.scalar_tensor_tensor(neg_logit[:], counts_g[:], weary_col[:], scores[:], ALU.mult, ALU.subtract)
        nc.scalar.activation(weights[:], neg_logit[:], ACT.Exp, bias=neg_lse[:], scale=-1.0)

        for c in range(4):
            nc.vector.memset(df[:, c * 512 : (c + 1) * 512], 0.0)

        grads = []
        for h in range(2):
            half_offsets = offsets[:, h * 16 : (h + 1) * 16]
            words_tag = ("first_words_then_second_bytes", "second_words")[h]
            bytes_tag = ("first_bytes", "first_words_then_second_bytes")[h]
            val_words_g = keep.tile([P, HALF], U32, name="val_words_g%d" % h, tag=words_tag, align_bytes=64)
            val_bytes_g = keep.tile([P, HALF], U8, name="val_bytes_g%d" % h, tag=bytes_tag, align_bytes=64)
            nc.vector.tensor_copy(val_words_g[:], val_words[:].indirect(half_offsets))
            nc.vector.tensor_copy(val_bytes_g[:], val_bytes[:].indirect(half_offsets))
            dp = psum.tile([P, HALF], F32, name="dp%d" % h)
            nc.tensor.matmul_mx(out=dp[:], lhsT=gout_codes[:].bitcast(FP8X4), lhsT_scale=gout_scales[:],
                                rhs=val_words_g[:].bitcast(FP8X4), rhs_scale=val_bytes_g[VALS_ROW:P, :],
                                start=True, stop=True)
            grad = keep.tile([P, HALF], F32, name="grad%d" % h)
            nc.scalar.activation(grad[:], dp[:], ACT.Identity, bias=shift[:], scale=factor[:])
            grads.append(grad)
        for h in range(2):
            nc.vector.tensor_tensor(df[:].indirect(offsets[:, h * 16 : (h + 1) * 16]), weights[:, h * HALF : (h + 1) * HALF], grads[h][:], ALU.mult)

        start = 0
        for c, width in enumerate(STORE_WIDTHS):
            cols = slice(start, start + width)
            result = keep.tile([P, width], F32, name="result%d" % c)
            nc.vector.tensor_tensor(result[:], later_all[:, cols], df[:, cols], ALU.add)
            nc.sync.dma_start(out[:, cols], result[:])
            start += width
